import numpy as np
import ml_dtypes


def mxq(x, axis, fmt="e4m3"):
    dtype, down = {"e4m3": (ml_dtypes.float8_e4m3fn, 7), "e5m2": (ml_dtypes.float8_e5m2, 14)}[fmt]
    v = np.moveaxis(np.asarray(x, np.float32).astype(ml_dtypes.bfloat16).astype(np.float64), axis, -1)
    blocks = v.reshape(v.shape[:-1] + (-1, 32))
    amax = np.abs(blocks).max(-1, keepdims=True)
    byte = np.maximum(np.where(amax > 0, np.frexp(amax)[1] - 1 + 127, 0) - down, 1)
    scale = np.exp2(byte - 127.0)
    codes = (blocks / scale).astype(np.float32).astype(dtype).astype(np.float64)
    return np.moveaxis((codes * scale).reshape(v.shape), -1, axis)


WIDE = False


def mx_kscale(k):
    if not WIDE:
        return np.ones(k)
    levels = np.array([10, -10, 5, -5, 0])
    if k % 512:
        return np.exp2(np.random.permutation(np.resize(levels, k // 32))).repeat(32)
    a = np.empty((k // 512, 16))
    for p in range(k // 512):
        a[p, :8] = np.random.permutation(np.resize(levels, 8))
        for g in range(8):
            far = levels[np.abs(levels - a[p, g]) >= 10]
            a[p, g + 8] = far[np.random.randint(len(far))]
    return np.exp2(a.ravel()).repeat(32)


def f64(x):
    return np.asarray(x).astype(np.float64)


def striped(idx):
    return np.tile(idx.reshape(-1, 16).T, (8, 1)).astype(np.uint16)


def unstriped(offs):
    return offs[:16].T.reshape(-1).astype(np.int64)


K, T, E, C, N = 1024, 1024, 8, 128, 256


def by_expert(wq, xq):
    return np.concatenate([wq[e].T @ xq[:, e * C:(e + 1) * C] for e in range(E)], axis=1)


def setup_inputs():
    n = np.random.standard_normal
    s = mx_kscale(K)[:, None]
    return {
        "xT": (n((K, T)) * s).astype(np.float32),
        "w": (n((E, K, N)) / np.sqrt(K) / s[None]).astype(np.float32),
        "gate": np.tile(np.random.uniform(0.2, 1.0, E * C), (N, 1)).astype(np.float32),
        "offs": striped(np.random.permutation(T)[:E * C]),
    }


def reference(xT, w, gate, offs):
    idx = unstriped(offs)
    xq = mxq(f64(xT)[:, idx], 0, "e4m3")
    y = by_expert(mxq(f64(w), 1, "e4m3"), xq)
    out = np.zeros((N, T))
    out[:, idx] = f64(gate) * y
    return out

@@ -1,0 +1,182 @@
+from contextlib import ExitStack
+
+import concourse.mybir as mybir
+
+K, T, E, C, N = 1024, 1024, 8, 128, 256
+FLOPS = 2 * K * N * E * C
+
+F32 = mybir.dt.float32
+BF16 = mybir.dt.bfloat16
+U32 = mybir.dt.uint32
+U16 = mybir.dt.uint16
+U8 = mybir.dt.uint8
+FP8X4 = mybir.dt.float8_e4m3fn_x4
+
+P = 128
+PACK = 4
+K_PASS = P * PACK
+PASSES = K // K_PASS
+M_TILE = 128
+BLOCKS = N // M_TILE
+HALF = 512
+HALVES = E * C // HALF
+LIST_COL = 16
+
+UNITS = ((0, 4), (4, 6), (6, 8))
+VECTOR_WEIGHTS = ()
+VECTOR_TOKENS = ()
+RING = 5
+EXTRA = (1, 2, 1, 2, 1, 2, 1, 0)
+
+
+def interleaved(dst, src):
+    return dst.rearrange("p (c i) j -> p c j i", i=4), src.rearrange("p j (c i) -> p c j i", i=4)
+
+
+def tile_routed_moe_kernel(tc, xT, w, gate, offs, out):
+    nc = tc.nc
+    mult = mybir.AluOpType.mult
+
+    with ExitStack() as ctx:
+        held = ctx.enter_context(tc.tile_pool(name="held", bufs=1))
+        ring = ctx.enter_context(tc.tile_pool(name="ring", bufs=RING))
+        psum = ctx.enter_context(tc.psum_pool(name="psum", bufs=1))
+
+        offsets = held.tile([P, E * C // LIST_COL], U16, name="offsets")
+        nc.sync.dma_start(offsets[:], offs)
+
+        x_view = xT.rearrange("(g p t) n -> g p t n", p=P, t=PACK)
+        w_view = w.rearrange("e (g p j) n -> e g p j n", p=P, j=PACK)
+
+        steps = []
+        pieces = [("weights", e, g) for e in range(E) for g in range(PASSES)]
+        for i in range(PASSES * PACK):
+            steps.append(("plane", i // PACK, i % PACK))
+            for r in range(EXTRA[i]):
+                steps.append(pieces.pop(0))
+        early = len(steps)
+        steps.extend([("gate", m, 0) for m in range(BLOCKS)])
+        steps.extend(pieces)
+
+        planes = {}
+        w_raw = {}
+        gate_sb = {}
+        for kind, a, b in steps:
+            if kind == "plane":
+                planes[a, b] = held.tile([P, T], F32, name="plane%d%d" % (a, b))
+                nc.sync.dma_start(planes[a, b][:], x_view[a, :, b, :])
+            elif kind == "weights":
+                w_raw[a, b] = held.tile([P, PACK, N], F32, name="w_raw%d%d" % (a, b))
+                nc.sync.dma_start(w_raw[a, b][:], w_view[a, b])
+            else:
+                gate_sb[a] = held.tile([P, E * C], F32, name="gate%d" % a)
+                nc.sync.dma_start(gate_sb[a][:], gate[a * M_TILE:(a + 1) * M_TILE, :])
+
+        picked = {}
+        x_grouped = {}
+        x_codes = {}
+        x_scales = {}
+        for g in range(PASSES):
+            for h in range(HALVES):
+                picked[g, h] = held.tile([P, PACK, HALF], F32, name="picked%d%d" % (g, h))
+                x_grouped[g, h] = held.tile([P, HALF, PACK], BF16, name="x_grouped%d%d" % (g, h), align_bytes=64)
+                x_codes[g, h] = held.tile([P, HALF], U32, name="x_codes%d%d" % (g, h), align_bytes=64)
+                x_scales[g, h] = held.tile([P, HALF], U8, name="x_scales%d%d" % (g, h), align_bytes=64)
+        w_grouped = {}
+        w_codes = {}
+        w_scales = {}
+        window = {}
+        for m in range(BLOCKS):
+            window[m] = held.tile([P, T], F32, name="window%d" % m)
+
+        def gather(g, t, h):
+            cols = HALF // LIST_COL
+            nc.vector.tensor_copy(
+                picked[g, h][:, t, :],
+                planes[g, t][:].indirect(offsets[:, h * cols:(h + 1) * cols]),
+            )
+
+        def interleave_tokens(g, h):
+            dst, src = interleaved(x_grouped[g, h][:], picked[g, h][:])
+            if (g, h) in VECTOR_TOKENS:
+                nc.vector.tensor_copy(out=dst, in_=src)
+            else:
+                nc.scalar.copy(out=dst, in_=src)
+
+        def quantize_tokens(g, h):
+            nc.vector.quantize_mx(
+                out=x_codes[g, h][:].bitcast(FP8X4),
+                scales=x_scales[g, h][:],
+                in_=x_grouped[g, h][:].rearrange("p n t -> p (n t)"),
+            )
+
+        def weights(e, g):
+            if g == 0:
+                w_grouped[e] = ring.tile([P, PASSES, N, PACK], BF16, name="w_grouped", align_bytes=64)
+            dst, src = interleaved(w_grouped[e][:, g, :, :], w_raw[e, g][:])
+            if (e, g) in VECTOR_WEIGHTS:
+                nc.vector.tensor_copy(out=dst, in_=src)
+            else:
+                nc.scalar.copy(out=dst, in_=src)
+            if g == PASSES - 1:
+                w_codes[e] = held.tile([P, PASSES * N], U32, name="w_codes%d" % e, align_bytes=64)
+                w_scales[e] = held.tile([P, PASSES * N], U8, name="w_scales%d" % e, align_bytes=64)
+                nc.vector.quantize_mx(
+                    out=w_codes[e][:].bitcast(FP8X4),
+                    scales=w_scales[e][:],
+                    in_=w_grouped[e][:].rearrange("p g n j -> p (g n j)"),
+                )
+
+        def finish(e0, e1, m):
+            slots = (e1 - e0) * C
+            acc = psum.tile([P, slots], F32, name="acc%d%d" % (e0, m))
+            for e in range(e0, e1):
+                h, col = (e * C) // HALF, (e * C) % HALF
+                for g in range(PASSES):
+                    first = g * N + m * M_TILE
+                    nc.tensor.matmul_mx(
+                        out=acc[:, (e - e0) * C:(e - e0 + 1) * C],
+                        lhsT=w_codes[e][:, first:first + M_TILE].bitcast(FP8X4),
+                        lhsT_scale=w_scales[e][:, first:first + M_TILE],
+                        rhs=x_codes[g, h][:, col:col + C].bitcast(FP8X4),
+                        rhs_scale=x_scales[g, h][:, col:col + C],
+                        start=(g == 0),
+                        stop=(g == PASSES - 1),
+                    )
+            sums = held.tile([P, slots], F32, name="sums%d%d" % (e0, m))
+            nc.scalar.copy(out=sums[:], in_=acc[:])
+            nc.vector.tensor_tensor(
+                out=window[m][:].indirect(offsets[:, e0 * C // LIST_COL:e1 * C // LIST_COL]),
+                in0=sums[:],
+                in1=gate_sb[m][:, e0 * C:e1 * C],
+                op=mult,
+            )
+            if e1 == E:
+                nc.sync.dma_start(out=out[m * M_TILE:(m + 1) * M_TILE, :], in_=window[m][:])
+
+        for kind, a, b in steps[:early]:
+            if kind == "plane":
+                for h in range(HALVES):
+                    gather(a, b, h)
+                if b == PACK - 1:
+                    for h in range(HALVES):
+                        interleave_tokens(a, h)
+                    for h in range(HALVES):
+                        quantize_tokens(a, h)
+            else:
+                weights(a, b)
+
+        late = [e for e in range(E) if e not in w_codes]
+        for e0, e1 in UNITS:
+            for m in range(BLOCKS):
+                while late and late[0] < e1:
+                    for g in range(PASSES):
+                        if g > 0 or late[0] not in w_grouped:
+                            weights(late[0], g)
+                    late.pop(0)
+                finish(e0, e1, m)
+                if late:
+                    for g in range(PASSES):
+                        if g > 0 or late[0] not in w_grouped:
+                            weights(late[0], g)
+                    late.pop(0)

@@ -18,15 +18,24 @@ K_PASS = P * PACK
 PASSES = K // K_PASS
 M_TILE = 128
 BLOCKS = N // M_TILE
-HALF = 512
-HALVES = E * C // HALF
+SLOTS = E * C
 LIST_COL = 16
 
 UNITS = ((0, 4), (4, 6), (6, 8))
+CHUNK = (512, 512)
+FINE = ()
+FINE_CUT = 256
+COARSE_CUT = 512
+SCALAR_PLANES = ((1, 3),)
+SCALAR_CUT = 512
+PLANE_ORDER = ((1, 3), (0, 0), (0, 1), (0, 2), (0, 3), (1, 0), (1, 1), (1, 2))
+EXTRA = (0, 0, 2, 2, 2, 2, 2, 0)
+GATE_AT = 0
 VECTOR_WEIGHTS = ()
 VECTOR_TOKENS = ()
 RING = 5
-EXTRA = (1, 2, 1, 2, 1, 2, 1, 0)
+WEAVE = 1
+SCALAR_CAST = True
 
 
 def interleaved(dst, src):
@@ -42,7 +51,7 @@ def tile_routed_moe_kernel(tc, xT, w, gate, offs, out):
         ring = ctx.enter_context(tc.tile_pool(name="ring", bufs=RING))
         psum = ctx.enter_context(tc.psum_pool(name="psum", bufs=1))
 
-        offsets = held.tile([P, E * C // LIST_COL], U16, name="offsets")
+        offsets = held.tile([P, SLOTS // LIST_COL], U16, name="offsets")
         nc.sync.dma_start(offsets[:], offs)
 
         x_view = xT.rearrange("(g p t) n -> g p t n", p=P, t=PACK)
@@ -51,12 +60,13 @@ def tile_routed_moe_kernel(tc, xT, w, gate, offs, out):
         steps = []
         pieces = [("weights", e, g) for e in range(E) for g in range(PASSES)]
         for i in range(PASSES * PACK):
-            steps.append(("plane", i // PACK, i % PACK))
+            steps.append(("plane", PLANE_ORDER[i][0], PLANE_ORDER[i][1]))
             for r in range(EXTRA[i]):
                 steps.append(pieces.pop(0))
         early = len(steps)
+        steps.extend(pieces[:GATE_AT])
         steps.extend([("gate", m, 0) for m in range(BLOCKS)])
-        steps.extend(pieces)
+        steps.extend(pieces[GATE_AT:])
 
         planes = {}
         w_raw = {}
@@ -69,19 +79,21 @@ def tile_routed_moe_kernel(tc, xT, w, gate, offs, out):
                 w_raw[a, b] = held.tile([P, PACK, N], F32, name="w_raw%d%d" % (a, b))
                 nc.sync.dma_start(w_raw[a, b][:], w_view[a, b])
             else:
-                gate_sb[a] = held.tile([P, E * C], F32, name="gate%d" % a)
+                gate_sb[a] = held.tile([P, SLOTS], F32, name="gate%d" % a)
                 nc.sync.dma_start(gate_sb[a][:], gate[a * M_TILE:(a + 1) * M_TILE, :])
 
+        vector_planes = {}
         picked = {}
         x_grouped = {}
         x_codes = {}
         x_scales = {}
         for g in range(PASSES):
-            for h in range(HALVES):
-                picked[g, h] = held.tile([P, PACK, HALF], F32, name="picked%d%d" % (g, h))
-                x_grouped[g, h] = held.tile([P, HALF, PACK], BF16, name="x_grouped%d%d" % (g, h), align_bytes=64)
-                x_codes[g, h] = held.tile([P, HALF], U32, name="x_codes%d%d" % (g, h), align_bytes=64)
-                x_scales[g, h] = held.tile([P, HALF], U8, name="x_scales%d%d" % (g, h), align_bytes=64)
+            vector_planes[g] = [t for t in range(PACK) if (g, t) not in SCALAR_PLANES]
+            picked[g] = held.tile([P, len(vector_planes[g]), SLOTS], F32, name="picked%d" % g)
+            for s in range(SLOTS // CHUNK[g]):
+                x_grouped[g, s] = held.tile([P, CHUNK[g], PACK], BF16, name="x_grouped%d%d" % (g, s), align_bytes=64)
+                x_codes[g, s] = held.tile([P, CHUNK[g]], U32, name="x_codes%d%d" % (g, s), align_bytes=64)
+                x_scales[g, s] = held.tile([P, CHUNK[g]], U8, name="x_scales%d%d" % (g, s), align_bytes=64)
         w_grouped = {}
         w_codes = {}
         w_scales = {}
@@ -89,25 +101,44 @@ def tile_routed_moe_kernel(tc, xT, w, gate, offs, out):
         for m in range(BLOCKS):
             window[m] = held.tile([P, T], F32, name="window%d" % m)
 
-        def gather(g, t, h):
-            cols = HALF // LIST_COL
-            nc.vector.tensor_copy(
-                picked[g, h][:, t, :],
-                planes[g, t][:].indirect(offsets[:, h * cols:(h + 1) * cols]),
-            )
+        def gather(g, t):
+            cut = FINE_CUT if (g, t) in FINE else COARSE_CUT
+            for first in range(0, SLOTS, cut):
+                nc.vector.tensor_copy(
+                    picked[g][:, t, first:first + cut],
+                    planes[g, t][:].indirect(offsets[:, first // LIST_COL:(first + cut) // LIST_COL]),
+                )
 
-        def interleave_tokens(g, h):
-            dst, src = interleaved(x_grouped[g, h][:], picked[g, h][:])
-            if (g, h) in VECTOR_TOKENS:
+        def scalar_gather(g, t):
+            rounded = held.tile([P, T], BF16, name="rounded%d%d" % (g, t))
+            if SCALAR_CAST:
+                nc.scalar.copy(out=rounded[:], in_=planes[g, t][:])
+            else:
+                nc.vector.tensor_copy(out=rounded[:], in_=planes[g, t][:])
+            cut = min(SCALAR_CUT, CHUNK[g])
+            for first in range(0, SLOTS, cut):
+                s, col = first // CHUNK[g], first % CHUNK[g]
+                nc.scalar.activation(
+                    x_grouped[g, s][:, col:col + cut, t],
+                    rounded[:].indirect(offsets[:, first // LIST_COL:(first + cut) // LIST_COL]),
+                    mybir.ActivationFunctionType.Copy,
+                )
+
+        def interleave_tokens(g, s):
+            dst, src = interleaved(
+                x_grouped[g, s][:, :, 0:len(vector_planes[g])],
+                picked[g][:, :, s * CHUNK[g]:(s + 1) * CHUNK[g]],
+            )
+            if (g, s) in VECTOR_TOKENS:
                 nc.vector.tensor_copy(out=dst, in_=src)
             else:
                 nc.scalar.copy(out=dst, in_=src)
 
-        def quantize_tokens(g, h):
+        def quantize_tokens(g, s):
             nc.vector.quantize_mx(
-                out=x_codes[g, h][:].bitcast(FP8X4),
-                scales=x_scales[g, h][:],
-                in_=x_grouped[g, h][:].rearrange("p n t -> p (n t)"),
+                out=x_codes[g, s][:].bitcast(FP8X4),
+                scales=x_scales[g, s][:],
+                in_=x_grouped[g, s][:].rearrange("p n t -> p (n t)"),
             )
 
         def weights(e, g):
@@ -131,15 +162,15 @@ def tile_routed_moe_kernel(tc, xT, w, gate, offs, out):
             slots = (e1 - e0) * C
             acc = psum.tile([P, slots], F32, name="acc%d%d" % (e0, m))
             for e in range(e0, e1):
-                h, col = (e * C) // HALF, (e * C) % HALF
                 for g in range(PASSES):
+                    s, col = (e * C) // CHUNK[g], (e * C) % CHUNK[g]
                     first = g * N + m * M_TILE
                     nc.tensor.matmul_mx(
                         out=acc[:, (e - e0) * C:(e - e0 + 1) * C],
                         lhsT=w_codes[e][:, first:first + M_TILE].bitcast(FP8X4),
                         lhsT_scale=w_scales[e][:, first:first + M_TILE],
-                        rhs=x_codes[g, h][:, col:col + C].bitcast(FP8X4),
-                        rhs_scale=x_scales[g, h][:, col:col + C],
+                        rhs=x_codes[g, s][:, col:col + C].bitcast(FP8X4),
+                        rhs_scale=x_scales[g, s][:, col:col + C],
                         start=(g == 0),
                         stop=(g == PASSES - 1),
                     )
@@ -154,29 +185,35 @@ def tile_routed_moe_kernel(tc, xT, w, gate, offs, out):
             if e1 == E:
                 nc.sync.dma_start(out=out[m * M_TILE:(m + 1) * M_TILE, :], in_=window[m][:])
 
+        seen = {0: 0, 1: 0}
         for kind, a, b in steps[:early]:
             if kind == "plane":
-                for h in range(HALVES):
-                    gather(a, b, h)
-                if b == PACK - 1:
-                    for h in range(HALVES):
-                        interleave_tokens(a, h)
-                    for h in range(HALVES):
-                        quantize_tokens(a, h)
+                if (a, b) in SCALAR_PLANES:
+                    scalar_gather(a, b)
+                else:
+                    gather(a, b)
+                seen[a] += 1
+                if seen[a] == PACK:
+                    for s in range(SLOTS // CHUNK[a]):
+                        interleave_tokens(a, s)
+                    for s in range(SLOTS // CHUNK[a]):
+                        quantize_tokens(a, s)
             else:
                 weights(a, b)
 
         late = [e for e in range(E) if e not in w_codes]
+
+        def next_weights():
+            for g in range(PASSES):
+                if g > 0 or late[0] not in w_grouped:
+                    weights(late[0], g)
+            late.pop(0)
+
         for e0, e1 in UNITS:
             for m in range(BLOCKS):
                 while late and late[0] < e1:
-                    for g in range(PASSES):
-                        if g > 0 or late[0] not in w_grouped:
-                            weights(late[0], g)
-                    late.pop(0)
+                    next_weights()
                 finish(e0, e1, m)
-                if late:
-                    for g in range(PASSES):
-                        if g > 0 or late[0] not in w_grouped:
-                            weights(late[0], g)
-                    late.pop(0)
+                for r in range(WEAVE):
+                    if late:
+                        next_weights()

@@ -35,7 +35,7 @@ VECTOR_WEIGHTS = ()
 VECTOR_TOKENS = ()
 RING = 5
 WEAVE = 1
-SCALAR_CAST = True
+SCALAR_CAST = False
 
 
 def interleaved(dst, src):

@@ -26,16 +26,17 @@ CHUNK = (512, 512)
 FINE = ()
 FINE_CUT = 256
 COARSE_CUT = 512
-SCALAR_PLANES = ((1, 3),)
+SCALAR_PLANES = ((0, 2), (0, 3), (1, 2), (1, 3))
 SCALAR_CUT = 512
-PLANE_ORDER = ((1, 3), (0, 0), (0, 1), (0, 2), (0, 3), (1, 0), (1, 1), (1, 2))
-EXTRA = (0, 0, 2, 2, 2, 2, 2, 0)
-GATE_AT = 0
-VECTOR_WEIGHTS = ()
-VECTOR_TOKENS = ()
+PLANE_ORDER = ((0, 2), (0, 0), (0, 3), (1, 2), (0, 1), (1, 3), (1, 0), (1, 1))
+EXTRA = (0, 0, 0, 0, 0, 0, 0, 0)
+GATE_AT = 4
+VECTOR_WEIGHTS = ((0, 0), (0, 1), (1, 0), (1, 1))
+VECTOR_TOKENS = ((0, 0), (0, 1))
 RING = 5
-WEAVE = 1
+WEAVE = 2
 SCALAR_CAST = False
+HALF = 512
 
 
 def interleaved(dst, src):
@@ -49,6 +50,7 @@ def tile_routed_moe_kernel(tc, xT, w, gate, offs, out):
     with ExitStack() as ctx:
         held = ctx.enter_context(tc.tile_pool(name="held", bufs=1))
         ring = ctx.enter_context(tc.tile_pool(name="ring", bufs=RING))
+        once = ctx.enter_context(tc.tile_pool(name="once", bufs=1))
         psum = ctx.enter_context(tc.psum_pool(name="psum", bufs=1))
 
         offsets = held.tile([P, SLOTS // LIST_COL], U16, name="offsets")
@@ -89,11 +91,13 @@ def tile_routed_moe_kernel(tc, xT, w, gate, offs, out):
         x_scales = {}
         for g in range(PASSES):
             vector_planes[g] = [t for t in range(PACK) if (g, t) not in SCALAR_PLANES]
-            picked[g] = held.tile([P, len(vector_planes[g]), SLOTS], F32, name="picked%d" % g)
+            if g == 0:
+                picked[g] = held.tile([P, len(vector_planes[g]), SLOTS], F32, name="picked%d" % g)
             for s in range(SLOTS // CHUNK[g]):
                 x_grouped[g, s] = held.tile([P, CHUNK[g], PACK], BF16, name="x_grouped%d%d" % (g, s), align_bytes=64)
                 x_codes[g, s] = held.tile([P, CHUNK[g]], U32, name="x_codes%d%d" % (g, s), align_bytes=64)
                 x_scales[g, s] = held.tile([P, CHUNK[g]], U8, name="x_scales%d%d" % (g, s), align_bytes=64)
+        late_picked = {}
         w_grouped = {}
         w_codes = {}
         w_scales = {}
@@ -108,6 +112,20 @@ def tile_routed_moe_kernel(tc, xT, w, gate, offs, out):
                     picked[g][:, t, first:first + cut],
                     planes[g, t][:].indirect(offsets[:, first // LIST_COL:(first + cut) // LIST_COL]),
                 )
+
+        def late_gather(t, h):
+            if h not in late_picked:
+                late_picked[h] = once.tile([P, len(vector_planes[1]), HALF], F32, name="late_picked")
+            first = h * HALF
+            nc.vector.tensor_copy(
+                late_picked[h][:, t, :],
+                planes[1, t][:].indirect(offsets[:, first // LIST_COL:(first + HALF) // LIST_COL]),
+            )
+
+        def late_tokens(h):
+            dst, src = interleaved(x_grouped[1, h][:, :, 0:len(vector_planes[1])], late_picked[h][:])
+            nc.vector.tensor_copy(out=dst, in_=src)
+            quantize_tokens(1, h)
 
         def scalar_gather(g, t):
             rounded = held.tile([P, T], BF16, name="rounded%d%d" % (g, t))
@@ -190,14 +208,21 @@ def tile_routed_moe_kernel(tc, xT, w, gate, offs, out):
             if kind == "plane":
                 if (a, b) in SCALAR_PLANES:
                     scalar_gather(a, b)
-                else:
+                elif a == 0:
                     gather(a, b)
+                else:
+                    late_gather(b, 0)
                 seen[a] += 1
-                if seen[a] == PACK:
+                if seen[a] == PACK and a == 0:
                     for s in range(SLOTS // CHUNK[a]):
                         interleave_tokens(a, s)
                     for s in range(SLOTS // CHUNK[a]):
                         quantize_tokens(a, s)
+                if seen[a] == PACK and a == 1:
+                    late_tokens(0)
+                    for t in vector_planes[1]:
+                        late_gather(t, 1)
+                    late_tokens(1)
             else:
                 weights(a, b)
 

@@ -34,9 +34,10 @@ GATE_AT = 4
 VECTOR_WEIGHTS = ((0, 0), (0, 1), (1, 0), (1, 1))
 VECTOR_TOKENS = ((0, 0), (0, 1))
 RING = 5
-WEAVE = 2
+WEAVE = 0
 SCALAR_CAST = False
 HALF = 512
+AHEAD = True
 
 
 def interleaved(dst, src):
@@ -176,7 +177,7 @@ def tile_routed_moe_kernel(tc, xT, w, gate, offs, out):
                     in_=w_grouped[e][:].rearrange("p g n j -> p (g n j)"),
                 )
 
-        def finish(e0, e1, m):
+        def finish(e0, e1, m, ahead):
             slots = (e1 - e0) * C
             acc = psum.tile([P, slots], F32, name="acc%d%d" % (e0, m))
             for e in range(e0, e1):
@@ -192,7 +193,7 @@ def tile_routed_moe_kernel(tc, xT, w, gate, offs, out):
                         start=(g == 0),
                         stop=(g == PASSES - 1),
                     )
-            sums = held.tile([P, slots], F32, name="sums%d%d" % (e0, m))
+            sums = held.tile([P, slots], F32, name=("w_raw%d%d" % (ahead, m) if ahead else "sums%d%d" % (e0, m)))
             nc.scalar.copy(out=sums[:], in_=acc[:])
             nc.vector.tensor_tensor(
                 out=window[m][:].indirect(offsets[:, e0 * C // LIST_COL:e1 * C // LIST_COL]),
@@ -234,11 +235,13 @@ def tile_routed_moe_kernel(tc, xT, w, gate, offs, out):
                     weights(late[0], g)
             late.pop(0)
 
-        for e0, e1 in UNITS:
+        for u in range(len(UNITS)):
+            e0, e1 = UNITS[u]
+            ahead = UNITS[u + 1][1] - 1 if AHEAD and u + 1 < len(UNITS) else 0
             for m in range(BLOCKS):
-                while late and late[0] < e1:
+                while late and late[0] < max(e1, ahead + 1):
                     next_weights()
-                finish(e0, e1, m)
+                finish(e0, e1, m, ahead)
                 for r in range(WEAVE):
                     if late:
                         next_weights()

@@ -55,7 +55,6 @@ def tile_routed_moe_kernel(tc, xT, w, gate, offs, out):
         psum = ctx.enter_context(tc.psum_pool(name="psum", bufs=1))
 
         offsets = held.tile([P, SLOTS // LIST_COL], U16, name="offsets")
-        nc.sync.dma_start(offsets[:], offs)
 
         x_view = xT.rearrange("(g p t) n -> g p t n", p=P, t=PACK)
         w_view = w.rearrange("e (g p j) n -> e g p j n", p=P, j=PACK)
@@ -78,6 +77,8 @@ def tile_routed_moe_kernel(tc, xT, w, gate, offs, out):
             if kind == "plane":
                 planes[a, b] = held.tile([P, T], F32, name="plane%d%d" % (a, b))
                 nc.sync.dma_start(planes[a, b][:], x_view[a, :, b, :])
+                if len(planes) == 1:
+                    nc.sync.dma_start(offsets[:], offs)
             elif kind == "weights":
                 w_raw[a, b] = held.tile([P, PACK, N], F32, name="w_raw%d%d" % (a, b))
                 nc.sync.dma_start(w_raw[a, b][:], w_view[a, b])

@@ -21,7 +21,7 @@ BLOCKS = N // M_TILE
 SLOTS = E * C
 LIST_COL = 16
 
-UNITS = ((0, 4), (4, 6), (6, 8))
+UNITS = ((0, 3), (3, 6), (6, 8))
 CHUNK = (512, 512)
 FINE = ()
 FINE_CUT = 256
@@ -35,7 +35,7 @@ VECTOR_WEIGHTS = ((0, 0), (0, 1), (1, 0), (1, 1))
 VECTOR_TOKENS = ((0, 0), (0, 1))
 RING = 5
 WEAVE = 0
-SCALAR_CAST = False
+SCALAR_CAST = ()
 HALF = 512
 AHEAD = True
 
@@ -131,7 +131,7 @@ def tile_routed_moe_kernel(tc, xT, w, gate, offs, out):
 
         def scalar_gather(g, t):
             rounded = held.tile([P, T], BF16, name="rounded%d%d" % (g, t))
-            if SCALAR_CAST:
+            if (g, t) in SCALAR_CAST:
                 nc.scalar.copy(out=rounded[:], in_=planes[g, t][:])
             else:
                 nc.vector.tensor_copy(out=rounded[:], in_=planes[g, t][:])

@@ -36,6 +36,7 @@ VECTOR_TOKENS = ((0, 0), (0, 1))
 RING = 5
 WEAVE = 0
 SCALAR_CAST = ()
+GPSIMD_CAST = ((1, 2), (1, 3))
 HALF = 512
 AHEAD = True
 
@@ -133,6 +134,8 @@ def tile_routed_moe_kernel(tc, xT, w, gate, offs, out):
             rounded = held.tile([P, T], BF16, name="rounded%d%d" % (g, t))
             if (g, t) in SCALAR_CAST:
                 nc.scalar.copy(out=rounded[:], in_=planes[g, t][:])
+            elif (g, t) in GPSIMD_CAST:
+                nc.gpsimd.tensor_copy(out=rounded[:], in_=planes[g, t][:])
             else:
                 nc.vector.tensor_copy(out=rounded[:], in_=planes[g, t][:])
             cut = min(SCALAR_CUT, CHUNK[g])

@@ -20,25 +20,20 @@ M_TILE = 128
 BLOCKS = N // M_TILE
 SLOTS = E * C
 LIST_COL = 16
-
-UNITS = ((0, 3), (3, 6), (6, 8))
-CHUNK = (512, 512)
-FINE = ()
-FINE_CUT = 256
-COARSE_CUT = 512
-SCALAR_PLANES = ((0, 2), (0, 3), (1, 2), (1, 3))
-SCALAR_CUT = 512
-PLANE_ORDER = ((0, 2), (0, 0), (0, 3), (1, 2), (0, 1), (1, 3), (1, 0), (1, 1))
-EXTRA = (0, 0, 0, 0, 0, 0, 0, 0)
-GATE_AT = 4
-VECTOR_WEIGHTS = ((0, 0), (0, 1), (1, 0), (1, 1))
-VECTOR_TOKENS = ((0, 0), (0, 1))
-RING = 5
-WEAVE = 0
-SCALAR_CAST = ()
-GPSIMD_CAST = ((1, 2), (1, 3))
 HALF = 512
-AHEAD = True
+HALVES = SLOTS // HALF
+
+UNITS = ((0, 2), (2, 4), (4, 6), (6, 7), (7, 8))
+SUMS_AT = (((3, 0), (3, 1)), ((4, 1), (5, 0)), ((6, 0), (6, 1)), ((7, 0), (7, 1)))
+AHEAD = (3, 5, 6, 7, 7)
+PLANES = ((0, 0), (0, 2), (0, 1), (0, 3), (1, 0), (1, 1), (1, 2), (1, 3))
+SCALAR_T = (2, 3)
+GPSIMD_CAST = ((0, 2), (0, 3), (1, 2), (1, 3))
+VECTOR_WEIGHTS = ((0, 0), (0, 1), (1, 0), (1, 1))
+GPSIMD_WEIGHTS = ()
+GATE_AT = 8
+LATE_AFTER = 0
+RING = 8
 
 
 def interleaved(dst, src):
@@ -52,7 +47,6 @@ def tile_routed_moe_kernel(tc, xT, w, gate, offs, out):
     with ExitStack() as ctx:
         held = ctx.enter_context(tc.tile_pool(name="held", bufs=1))
         ring = ctx.enter_context(tc.tile_pool(name="ring", bufs=RING))
-        once = ctx.enter_context(tc.tile_pool(name="once", bufs=1))
         psum = ctx.enter_context(tc.psum_pool(name="psum", bufs=1))
 
         offsets = held.tile([P, SLOTS // LIST_COL], U16, name="offsets")
@@ -60,47 +54,33 @@ def tile_routed_moe_kernel(tc, xT, w, gate, offs, out):
         x_view = xT.rearrange("(g p t) n -> g p t n", p=P, t=PACK)
         w_view = w.rearrange("e (g p j) n -> e g p j n", p=P, j=PACK)
 
-        steps = []
-        pieces = [("weights", e, g) for e in range(E) for g in range(PASSES)]
-        for i in range(PASSES * PACK):
-            steps.append(("plane", PLANE_ORDER[i][0], PLANE_ORDER[i][1]))
-            for r in range(EXTRA[i]):
-                steps.append(pieces.pop(0))
-        early = len(steps)
-        steps.extend(pieces[:GATE_AT])
-        steps.extend([("gate", m, 0) for m in range(BLOCKS)])
-        steps.extend(pieces[GATE_AT:])
-
         planes = {}
+        for g, t in PLANES:
+            planes[g, t] = held.tile([P, T], F32, name="plane%d%d" % (g, t))
+            nc.sync.dma_start(planes[g, t][:], x_view[g, :, t, :])
+            if len(planes) == 1:
+                nc.sync.dma_start(offsets[:], offs)
         w_raw = {}
         gate_sb = {}
-        for kind, a, b in steps:
-            if kind == "plane":
-                planes[a, b] = held.tile([P, T], F32, name="plane%d%d" % (a, b))
-                nc.sync.dma_start(planes[a, b][:], x_view[a, :, b, :])
-                if len(planes) == 1:
-                    nc.sync.dma_start(offsets[:], offs)
-            elif kind == "weights":
-                w_raw[a, b] = held.tile([P, PACK, N], F32, name="w_raw%d%d" % (a, b))
-                nc.sync.dma_start(w_raw[a, b][:], w_view[a, b])
-            else:
-                gate_sb[a] = held.tile([P, SLOTS], F32, name="gate%d" % a)
-                nc.sync.dma_start(gate_sb[a][:], gate[a * M_TILE:(a + 1) * M_TILE, :])
+        pieces = [(e, g) for e in range(E) for g in range(PASSES)]
+        for i in range(len(pieces)):
+            if i == GATE_AT:
+                for m in range(BLOCKS):
+                    gate_sb[m] = held.tile([P, SLOTS], F32, name="gate%d" % m)
+                    nc.sync.dma_start(gate_sb[m][:], gate[m * M_TILE:(m + 1) * M_TILE, :])
+            e, g = pieces[i]
+            w_raw[e, g] = held.tile([P, PACK, N], F32, name="w_raw%d%d" % (e, g), align_bytes=64)
+            nc.sync.dma_start(w_raw[e, g][:], w_view[e, g])
 
-        vector_planes = {}
-        picked = {}
         x_grouped = {}
+        picked = {}
         x_codes = {}
         x_scales = {}
         for g in range(PASSES):
-            vector_planes[g] = [t for t in range(PACK) if (g, t) not in SCALAR_PLANES]
-            if g == 0:
-                picked[g] = held.tile([P, len(vector_planes[g]), SLOTS], F32, name="picked%d" % g)
-            for s in range(SLOTS // CHUNK[g]):
-                x_grouped[g, s] = held.tile([P, CHUNK[g], PACK], BF16, name="x_grouped%d%d" % (g, s), align_bytes=64)
-                x_codes[g, s] = held.tile([P, CHUNK[g]], U32, name="x_codes%d%d" % (g, s), align_bytes=64)
-                x_scales[g, s] = held.tile([P, CHUNK[g]], U8, name="x_scales%d%d" % (g, s), align_bytes=64)
-        late_picked = {}
+            for h in range(HALVES):
+                x_grouped[g, h] = held.tile([P, HALF, PACK], BF16, name="x_grouped%d%d" % (g, h), align_bytes=64)
+                picked[g, h] = held.tile([P, PACK - len(SCALAR_T), HALF], F32, name="picked%d%d" % (g, h))
+                x_scales[g, h] = held.tile([P, HALF], U8, name="x_scales%d%d" % (g, h), align_bytes=64)
         w_grouped = {}
         w_codes = {}
         w_scales = {}
@@ -108,96 +88,78 @@ def tile_routed_moe_kernel(tc, xT, w, gate, offs, out):
         for m in range(BLOCKS):
             window[m] = held.tile([P, T], F32, name="window%d" % m)
 
-        def gather(g, t):
-            cut = FINE_CUT if (g, t) in FINE else COARSE_CUT
-            for first in range(0, SLOTS, cut):
-                nc.vector.tensor_copy(
-                    picked[g][:, t, first:first + cut],
-                    planes[g, t][:].indirect(offsets[:, first // LIST_COL:(first + cut) // LIST_COL]),
-                )
+        def half_list(h):
+            return offsets[:, h * HALF // LIST_COL:(h + 1) * HALF // LIST_COL]
 
-        def late_gather(t, h):
-            if h not in late_picked:
-                late_picked[h] = once.tile([P, len(vector_planes[1]), HALF], F32, name="late_picked")
-            first = h * HALF
-            nc.vector.tensor_copy(
-                late_picked[h][:, t, :],
-                planes[1, t][:].indirect(offsets[:, first // LIST_COL:(first + HALF) // LIST_COL]),
-            )
-
-        def late_tokens(h):
-            dst, src = interleaved(x_grouped[1, h][:, :, 0:len(vector_planes[1])], late_picked[h][:])
-            nc.vector.tensor_copy(out=dst, in_=src)
-            quantize_tokens(1, h)
-
-        def scalar_gather(g, t):
+        def scalar_plane(g, t):
             rounded = held.tile([P, T], BF16, name="rounded%d%d" % (g, t))
-            if (g, t) in SCALAR_CAST:
-                nc.scalar.copy(out=rounded[:], in_=planes[g, t][:])
-            elif (g, t) in GPSIMD_CAST:
+            if (g, t) in GPSIMD_CAST:
                 nc.gpsimd.tensor_copy(out=rounded[:], in_=planes[g, t][:])
             else:
                 nc.vector.tensor_copy(out=rounded[:], in_=planes[g, t][:])
-            cut = min(SCALAR_CUT, CHUNK[g])
-            for first in range(0, SLOTS, cut):
-                s, col = first // CHUNK[g], first % CHUNK[g]
+            for h in range(HALVES):
                 nc.scalar.activation(
-                    x_grouped[g, s][:, col:col + cut, t],
-                    rounded[:].indirect(offsets[:, first // LIST_COL:(first + cut) // LIST_COL]),
+                    x_grouped[g, h][:, :, t],
+                    rounded[:].indirect(half_list(h)),
                     mybir.ActivationFunctionType.Copy,
                 )
 
-        def interleave_tokens(g, s):
-            dst, src = interleaved(
-                x_grouped[g, s][:, :, 0:len(vector_planes[g])],
-                picked[g][:, :, s * CHUNK[g]:(s + 1) * CHUNK[g]],
-            )
-            if (g, s) in VECTOR_TOKENS:
-                nc.vector.tensor_copy(out=dst, in_=src)
-            else:
-                nc.scalar.copy(out=dst, in_=src)
+        def vector_plane(g, t):
+            for h in range(HALVES):
+                nc.vector.tensor_copy(picked[g, h][:, t, :], planes[g, t][:].indirect(half_list(h)))
 
-        def quantize_tokens(g, s):
+        def interleave_tokens(g, h):
+            dst, src = interleaved(x_grouped[g, h][:, :, 0:PACK - len(SCALAR_T)], picked[g, h][:])
+            nc.vector.tensor_copy(out=dst, in_=src)
+
+        def quantize_tokens(g, h, name):
+            x_codes[g, h] = held.tile([P, HALF], U32, name=name, align_bytes=64)
             nc.vector.quantize_mx(
-                out=x_codes[g, s][:].bitcast(FP8X4),
-                scales=x_scales[g, s][:],
-                in_=x_grouped[g, s][:].rearrange("p n t -> p (n t)"),
+                out=x_codes[g, h][:].bitcast(FP8X4),
+                scales=x_scales[g, h][:],
+                in_=x_grouped[g, h][:].rearrange("p n t -> p (n t)"),
             )
 
-        def weights(e, g):
-            if g == 0:
-                w_grouped[e] = ring.tile([P, PASSES, N, PACK], BF16, name="w_grouped", align_bytes=64)
-            dst, src = interleaved(w_grouped[e][:, g, :, :], w_raw[e, g][:])
-            if (e, g) in VECTOR_WEIGHTS:
-                nc.vector.tensor_copy(out=dst, in_=src)
+        def weights(e):
+            if e == LATE_AFTER:
+                w_grouped[e] = held.tile([P, PASSES, N, PACK], BF16, name="w_grouped%d" % e, align_bytes=64)
             else:
-                nc.scalar.copy(out=dst, in_=src)
-            if g == PASSES - 1:
-                w_codes[e] = held.tile([P, PASSES * N], U32, name="w_codes%d" % e, align_bytes=64)
-                w_scales[e] = held.tile([P, PASSES * N], U8, name="w_scales%d" % e, align_bytes=64)
-                nc.vector.quantize_mx(
-                    out=w_codes[e][:].bitcast(FP8X4),
-                    scales=w_scales[e][:],
-                    in_=w_grouped[e][:].rearrange("p g n j -> p (g n j)"),
-                )
+                w_grouped[e] = ring.tile([P, PASSES, N, PACK], BF16, name="w_grouped", align_bytes=64)
+            for g in range(PASSES):
+                dst, src = interleaved(w_grouped[e][:, g, :, :], w_raw[e, g][:])
+                if (e, g) in VECTOR_WEIGHTS:
+                    nc.vector.tensor_copy(out=dst, in_=src)
+                elif (e, g) in GPSIMD_WEIGHTS:
+                    nc.gpsimd.tensor_copy(out=w_grouped[e][:, g, :, :], in_=w_raw[e, g][:].rearrange("p j n -> p n j"))
+                else:
+                    nc.scalar.copy(out=dst, in_=src)
+            w_codes[e] = held.tile([P, PASSES * N], U32, name="w_codes%d" % e, align_bytes=64)
+            w_scales[e] = held.tile([P, PASSES * N], U8, name="w_scales%d" % e, align_bytes=64)
+            nc.vector.quantize_mx(
+                out=w_codes[e][:].bitcast(FP8X4),
+                scales=w_scales[e][:],
+                in_=w_grouped[e][:].rearrange("p g n j -> p (g n j)"),
+            )
 
-        def finish(e0, e1, m, ahead):
+        def finish(u, m):
+            e0, e1 = UNITS[u]
             slots = (e1 - e0) * C
-            acc = psum.tile([P, slots], F32, name="acc%d%d" % (e0, m))
+            acc = psum.tile([P, slots], F32, name="acc%d%d" % (u % 4, m))
             for e in range(e0, e1):
                 for g in range(PASSES):
-                    s, col = (e * C) // CHUNK[g], (e * C) % CHUNK[g]
+                    h, col = (e * C) // HALF, (e * C) % HALF
                     first = g * N + m * M_TILE
                     nc.tensor.matmul_mx(
                         out=acc[:, (e - e0) * C:(e - e0 + 1) * C],
                         lhsT=w_codes[e][:, first:first + M_TILE].bitcast(FP8X4),
                         lhsT_scale=w_scales[e][:, first:first + M_TILE],
-                        rhs=x_codes[g, s][:, col:col + C].bitcast(FP8X4),
-                        rhs_scale=x_scales[g, s][:, col:col + C],
+                        rhs=x_codes[g, h][:, col:col + C].bitcast(FP8X4),
+                        rhs_scale=x_scales[g, h][:, col:col + C],
                         start=(g == 0),
                         stop=(g == PASSES - 1),
                     )
-            sums = held.tile([P, slots], F32, name=("w_raw%d%d" % (ahead, m) if ahead else "sums%d%d" % (e0, m)))
+            name = "w_raw%d%d" % SUMS_AT[u][m] if u < len(SUMS_AT) else "sums%d" % m
+            sums = held.tile([P, slots], F32, name=name, align_bytes=64)
             nc.scalar.copy(out=sums[:], in_=acc[:])
             nc.vector.tensor_tensor(
                 out=window[m][:].indirect(offsets[:, e0 * C // LIST_COL:e1 * C // LIST_COL]),
@@ -208,44 +170,29 @@ def tile_routed_moe_kernel(tc, xT, w, gate, offs, out):
             if e1 == E:
                 nc.sync.dma_start(out=out[m * M_TILE:(m + 1) * M_TILE, :], in_=window[m][:])
 
-        seen = {0: 0, 1: 0}
-        for kind, a, b in steps[:early]:
-            if kind == "plane":
-                if (a, b) in SCALAR_PLANES:
-                    scalar_gather(a, b)
-                elif a == 0:
-                    gather(a, b)
-                else:
-                    late_gather(b, 0)
-                seen[a] += 1
-                if seen[a] == PACK and a == 0:
-                    for s in range(SLOTS // CHUNK[a]):
-                        interleave_tokens(a, s)
-                    for s in range(SLOTS // CHUNK[a]):
-                        quantize_tokens(a, s)
-                if seen[a] == PACK and a == 1:
-                    late_tokens(0)
-                    for t in vector_planes[1]:
-                        late_gather(t, 1)
-                    late_tokens(1)
+        vector_left = {g: PACK - len(SCALAR_T) for g in range(PASSES)}
+        left = {g: PACK for g in range(PASSES)}
+        for g, t in PLANES:
+            if t in SCALAR_T:
+                scalar_plane(g, t)
             else:
-                weights(a, b)
+                vector_plane(g, t)
+                vector_left[g] -= 1
+                if vector_left[g] == 0:
+                    for h in range(HALVES):
+                        interleave_tokens(g, h)
+            left[g] -= 1
+            if left[g] == 0 and g == 0:
+                for h in range(HALVES):
+                    quantize_tokens(g, h, "x_codes%d%d" % (g, h))
 
-        late = [e for e in range(E) if e not in w_codes]
-
-        def next_weights():
-            for g in range(PASSES):
-                if g > 0 or late[0] not in w_grouped:
-                    weights(late[0], g)
-            late.pop(0)
-
+        done = 0
         for u in range(len(UNITS)):
-            e0, e1 = UNITS[u]
-            ahead = UNITS[u + 1][1] - 1 if AHEAD and u + 1 < len(UNITS) else 0
+            while done <= AHEAD[u]:
+                weights(done)
+                if done == LATE_AFTER:
+                    quantize_tokens(1, 0, "w_grouped%d" % done)
+                    quantize_tokens(1, 1, "w_raw%d%d" % (done, PASSES - 1))
+                done += 1
             for m in range(BLOCKS):
-                while late and late[0] < max(e1, ahead + 1):
-                    next_weights()
-                finish(e0, e1, m, ahead)
-                for r in range(WEAVE):
-                    if late:
-                        next_weights()
+                finish(u, m)

@@ -23,16 +23,16 @@ LIST_COL = 16
 HALF = 512
 HALVES = SLOTS // HALF
 
-UNITS = ((0, 2), (2, 4), (4, 6), (6, 7), (7, 8))
-SUMS_AT = (((3, 0), (3, 1)), ((4, 1), (5, 0)), ((6, 0), (6, 1)), ((7, 0), (7, 1)))
-AHEAD = (3, 5, 6, 7, 7)
-PLANES = ((0, 0), (0, 2), (0, 1), (0, 3), (1, 0), (1, 1), (1, 2), (1, 3))
-SCALAR_T = (2, 3)
-GPSIMD_CAST = ((0, 2), (0, 3), (1, 2), (1, 3))
-VECTOR_WEIGHTS = ((0, 0), (0, 1), (1, 0), (1, 1))
+UNITS = ((0, 2), (2, 4), (4, 6), (6, 8))
+SUMS_AT = (6, 8, 14, 16)
+PLANES = ((0, 0), (1, 0), (0, 1), (1, 1), (0, 2), (1, 2), (0, 3), (1, 3))
+SCALAR_PASS = 1
+GPSIMD_CAST = ((1, 0), (1, 1), (1, 2), (1, 3))
+VECTOR_WEIGHTS = ((0, 0), (0, 1), (1, 0), (1, 1), (2, 0))
 GPSIMD_WEIGHTS = ()
 GATE_AT = 8
-LATE_AFTER = 0
+LATE_AT = ((1, "w_raw01"), (3, "w_grouped1"))
+EARLY_EXPERTS = (0, 1)
 RING = 8
 
 
@@ -79,7 +79,8 @@ def tile_routed_moe_kernel(tc, xT, w, gate, offs, out):
         for g in range(PASSES):
             for h in range(HALVES):
                 x_grouped[g, h] = held.tile([P, HALF, PACK], BF16, name="x_grouped%d%d" % (g, h), align_bytes=64)
-                picked[g, h] = held.tile([P, PACK - len(SCALAR_T), HALF], F32, name="picked%d%d" % (g, h))
+                if g != SCALAR_PASS:
+                    picked[g, h] = held.tile([P, PACK, HALF], F32, name="picked%d%d" % (g, h))
                 x_scales[g, h] = held.tile([P, HALF], U8, name="x_scales%d%d" % (g, h), align_bytes=64)
         w_grouped = {}
         w_codes = {}
@@ -109,7 +110,7 @@ def tile_routed_moe_kernel(tc, xT, w, gate, offs, out):
                 nc.vector.tensor_copy(picked[g, h][:, t, :], planes[g, t][:].indirect(half_list(h)))
 
         def interleave_tokens(g, h):
-            dst, src = interleaved(x_grouped[g, h][:, :, 0:PACK - len(SCALAR_T)], picked[g, h][:])
+            dst, src = interleaved(x_grouped[g, h][:], picked[g, h][:])
             nc.vector.tensor_copy(out=dst, in_=src)
 
         def quantize_tokens(g, h, name):
@@ -120,26 +121,27 @@ def tile_routed_moe_kernel(tc, xT, w, gate, offs, out):
                 in_=x_grouped[g, h][:].rearrange("p n t -> p (n t)"),
             )
 
-        def weights(e):
-            if e == LATE_AFTER:
-                w_grouped[e] = held.tile([P, PASSES, N, PACK], BF16, name="w_grouped%d" % e, align_bytes=64)
-            else:
-                w_grouped[e] = ring.tile([P, PASSES, N, PACK], BF16, name="w_grouped", align_bytes=64)
-            for g in range(PASSES):
-                dst, src = interleaved(w_grouped[e][:, g, :, :], w_raw[e, g][:])
-                if (e, g) in VECTOR_WEIGHTS:
-                    nc.vector.tensor_copy(out=dst, in_=src)
-                elif (e, g) in GPSIMD_WEIGHTS:
-                    nc.gpsimd.tensor_copy(out=w_grouped[e][:, g, :, :], in_=w_raw[e, g][:].rearrange("p j n -> p n j"))
+        def weights(e, g):
+            if g == 0:
+                if e in EARLY_EXPERTS:
+                    w_grouped[e] = held.tile([P, PASSES, N, PACK], BF16, name="w_grouped%d" % e, align_bytes=64)
                 else:
-                    nc.scalar.copy(out=dst, in_=src)
-            w_codes[e] = held.tile([P, PASSES * N], U32, name="w_codes%d" % e, align_bytes=64)
-            w_scales[e] = held.tile([P, PASSES * N], U8, name="w_scales%d" % e, align_bytes=64)
-            nc.vector.quantize_mx(
-                out=w_codes[e][:].bitcast(FP8X4),
-                scales=w_scales[e][:],
-                in_=w_grouped[e][:].rearrange("p g n j -> p (g n j)"),
-            )
+                    w_grouped[e] = ring.tile([P, PASSES, N, PACK], BF16, name="w_grouped", align_bytes=64)
+            dst, src = interleaved(w_grouped[e][:, g, :, :], w_raw[e, g][:])
+            if (e, g) in VECTOR_WEIGHTS:
+                nc.vector.tensor_copy(out=dst, in_=src)
+            elif (e, g) in GPSIMD_WEIGHTS:
+                nc.gpsimd.tensor_copy(out=w_grouped[e][:, g, :, :], in_=w_raw[e, g][:].rearrange("p j n -> p n j"))
+            else:
+                nc.scalar.copy(out=dst, in_=src)
+            if g == PASSES - 1:
+                w_codes[e] = held.tile([P, PASSES * N], U32, name="w_codes%d" % e, align_bytes=64)
+                w_scales[e] = held.tile([P, PASSES * N], U8, name="w_scales%d" % e, align_bytes=64)
+                nc.vector.quantize_mx(
+                    out=w_codes[e][:].bitcast(FP8X4),
+                    scales=w_scales[e][:],
+                    in_=w_grouped[e][:].rearrange("p g n j -> p (g n j)"),
+                )
 
         def finish(u, m):
             e0, e1 = UNITS[u]
@@ -158,7 +160,8 @@ def tile_routed_moe_kernel(tc, xT, w, gate, offs, out):
                         start=(g == 0),
                         stop=(g == PASSES - 1),
                     )
-            name = "w_raw%d%d" % SUMS_AT[u][m] if u < len(SUMS_AT) else "sums%d" % m
+            at = SUMS_AT[u] + m
+            name = "w_raw%d%d" % pieces[at] if at < len(pieces) else "sums%d" % m
             sums = held.tile([P, slots], F32, name=name, align_bytes=64)
             nc.scalar.copy(out=sums[:], in_=acc[:])
             nc.vector.tensor_tensor(
@@ -170,29 +173,24 @@ def tile_routed_moe_kernel(tc, xT, w, gate, offs, out):
             if e1 == E:
                 nc.sync.dma_start(out=out[m * M_TILE:(m + 1) * M_TILE, :], in_=window[m][:])
 
-        vector_left = {g: PACK - len(SCALAR_T) for g in range(PASSES)}
-        left = {g: PACK for g in range(PASSES)}
         for g, t in PLANES:
-            if t in SCALAR_T:
+            if g == SCALAR_PASS:
                 scalar_plane(g, t)
             else:
                 vector_plane(g, t)
-                vector_left[g] -= 1
-                if vector_left[g] == 0:
-                    for h in range(HALVES):
-                        interleave_tokens(g, h)
-            left[g] -= 1
-            if left[g] == 0 and g == 0:
-                for h in range(HALVES):
-                    quantize_tokens(g, h, "x_codes%d%d" % (g, h))
+        for h in range(HALVES):
+            interleave_tokens(0, h)
+        for h in range(HALVES):
+            quantize_tokens(0, h, "x_codes0%d" % h)
 
-        done = 0
-        for u in range(len(UNITS)):
-            while done <= AHEAD[u]:
-                weights(done)
-                if done == LATE_AFTER:
-                    quantize_tokens(1, 0, "w_grouped%d" % done)
-                    quantize_tokens(1, 1, "w_raw%d%d" % (done, PASSES - 1))
-                done += 1
-            for m in range(BLOCKS):
-                finish(u, m)
+        for i in range(len(pieces) + BLOCKS):
+            if i < len(pieces):
+                e, g = pieces[i]
+                weights(e, g)
+            for h in range(HALVES):
+                if LATE_AT[h][0] == i:
+                    quantize_tokens(1, h, LATE_AT[h][1])
+            for u in range(len(UNITS)):
+                for m in range(BLOCKS):
+                    if SUMS_AT[u] + m == i:
+                        finish(u, m)

@@ -23,14 +23,15 @@ LIST_COL = 16
 HALF = 512
 HALVES = SLOTS // HALF
 
-UNITS = ((0, 2), (2, 4), (4, 6), (6, 8))
-SUMS_AT = (6, 8, 14, 16)
+UNITS = ((0, 2), (2, 4), (4, 6), (6, 7), (7, 8))
+SUMS_AT = (6, 9, 12, 14, 16)
 PLANES = ((0, 0), (1, 0), (0, 1), (1, 1), (0, 2), (1, 2), (0, 3), (1, 3))
 SCALAR_PASS = 1
 GPSIMD_CAST = ((1, 0), (1, 1), (1, 2), (1, 3))
 VECTOR_WEIGHTS = ((0, 0), (0, 1), (1, 0), (1, 1), (2, 0))
 GPSIMD_WEIGHTS = ()
-GATE_AT = 8
+SCALAR_SHARE = {(1, 0): 512}
+GATE_AT = (8, 12)
 LATE_AT = ((1, "w_raw01"), (3, "w_grouped1"))
 EARLY_EXPERTS = (0, 1)
 RING = 8
@@ -55,22 +56,27 @@ def tile_routed_moe_kernel(tc, xT, w, gate, offs, out):
         w_view = w.rearrange("e (g p j) n -> e g p j n", p=P, j=PACK)
 
         planes = {}
-        for g, t in PLANES:
-            planes[g, t] = held.tile([P, T], F32, name="plane%d%d" % (g, t))
-            nc.sync.dma_start(planes[g, t][:], x_view[g, :, t, :])
-            if len(planes) == 1:
-                nc.sync.dma_start(offsets[:], offs)
         w_raw = {}
         gate_sb = {}
         pieces = [(e, g) for e in range(E) for g in range(PASSES)]
+        order = [("x",) + p for p in PLANES]
         for i in range(len(pieces)):
-            if i == GATE_AT:
-                for m in range(BLOCKS):
-                    gate_sb[m] = held.tile([P, SLOTS], F32, name="gate%d" % m)
-                    nc.sync.dma_start(gate_sb[m][:], gate[m * M_TILE:(m + 1) * M_TILE, :])
-            e, g = pieces[i]
-            w_raw[e, g] = held.tile([P, PACK, N], F32, name="w_raw%d%d" % (e, g), align_bytes=64)
-            nc.sync.dma_start(w_raw[e, g][:], w_view[e, g])
+            for h in range(HALVES):
+                if i == GATE_AT[h]:
+                    order.extend([("gate", m, h) for m in range(BLOCKS)])
+            order.append(("w",) + pieces[i])
+        for kind, a, b in order:
+            if kind == "x":
+                planes[a, b] = held.tile([P, T], F32, name="plane%d%d" % (a, b))
+                nc.sync.dma_start(planes[a, b][:], x_view[a, :, b, :])
+                if len(planes) == 1:
+                    nc.sync.dma_start(offsets[:], offs)
+            elif kind == "w":
+                w_raw[a, b] = held.tile([P, PACK, N], F32, name="w_raw%d%d" % (a, b), align_bytes=64)
+                nc.sync.dma_start(w_raw[a, b][:], w_view[a, b])
+            else:
+                gate_sb[a, b] = held.tile([P, HALF], F32, name="gate%d%d" % (a, b))
+                nc.sync.dma_start(gate_sb[a, b][:], gate[a * M_TILE:(a + 1) * M_TILE, b * HALF:(b + 1) * HALF])
 
         x_grouped = {}
         picked = {}
@@ -94,10 +100,11 @@ def tile_routed_moe_kernel(tc, xT, w, gate, offs, out):
 
         def scalar_plane(g, t):
             rounded = held.tile([P, T], BF16, name="rounded%d%d" % (g, t))
-            if (g, t) in GPSIMD_CAST:
-                nc.gpsimd.tensor_copy(out=rounded[:], in_=planes[g, t][:])
-            else:
-                nc.vector.tensor_copy(out=rounded[:], in_=planes[g, t][:])
+            cut = T - SCALAR_SHARE.get((g, t), 0)
+            if cut > 0:
+                nc.gpsimd.tensor_copy(out=rounded[:, 0:cut], in_=planes[g, t][:, 0:cut])
+            if cut < T:
+                nc.scalar.copy(out=rounded[:, cut:T], in_=planes[g, t][:, cut:T])
             for h in range(HALVES):
                 nc.scalar.activation(
                     x_grouped[g, h][:, :, t],
@@ -167,7 +174,7 @@ def tile_routed_moe_kernel(tc, xT, w, gate, offs, out):
             nc.vector.tensor_tensor(
                 out=window[m][:].indirect(offsets[:, e0 * C // LIST_COL:e1 * C // LIST_COL]),
                 in0=sums[:],
-                in1=gate_sb[m][:, e0 * C:e1 * C],
+                in1=gate_sb[m, e0 * C // HALF][:, e0 * C % HALF:e0 * C % HALF + slots],
                 op=mult,
             )
             if e1 == E:

@@ -24,17 +24,17 @@ HALF = 512
 HALVES = SLOTS // HALF
 
 UNITS = ((0, 2), (2, 4), (4, 6), (6, 7), (7, 8))
-SUMS_AT = (6, 9, 12, 14, 16)
+GROUPS = ((0, 2), (2, 4), (4, 6), (6, 7), (7, 8))
+SUMS_AT = ((6, 7), (9, 11), (12, 13), (14, 15), (16, 17))
 PLANES = ((0, 0), (1, 0), (0, 1), (1, 1), (0, 2), (1, 2), (0, 3), (1, 3))
-SCALAR_PASS = 1
-GPSIMD_CAST = ((1, 0), (1, 1), (1, 2), (1, 3))
-VECTOR_WEIGHTS = ((0, 0), (0, 1), (1, 0), (1, 1), (2, 0))
-GPSIMD_WEIGHTS = ()
 SCALAR_SHARE = {(1, 0): 512}
+WHOLE_EXPERTS = (0, 1)
+VECTOR_PIECES = ((2, 0),)
 GATE_AT = (8, 12)
-LATE_AT = ((1, "w_raw01"), (3, "w_grouped1"))
-EARLY_EXPERTS = (0, 1)
-RING = 8
+LATE_AT = ((3, "w_raw1"),)
+LONG_GATHERS = True
+TOKEN_CUTS = ((0, 1024),)
+LATE_CUTS = ((0, 512), (512, 1024))
 
 
 def interleaved(dst, src):
@@ -47,7 +47,6 @@ def tile_routed_moe_kernel(tc, xT, w, gate, offs, out):
 
     with ExitStack() as ctx:
         held = ctx.enter_context(tc.tile_pool(name="held", bufs=1))
-        ring = ctx.enter_context(tc.tile_pool(name="ring", bufs=RING))
         psum = ctx.enter_context(tc.psum_pool(name="psum", bufs=1))
 
         offsets = held.tile([P, SLOTS // LIST_COL], U16, name="offsets")
@@ -55,7 +54,8 @@ def tile_routed_moe_kernel(tc, xT, w, gate, offs, out):
         x_view = xT.rearrange("(g p t) n -> g p t n", p=P, t=PACK)
         w_view = w.rearrange("e (g p j) n -> e g p j n", p=P, j=PACK)
 
-        planes = {}
+        vector_planes = held.tile([P, PACK, T], F32, name="vector_planes")
+        scalar_planes = {}
         w_raw = {}
         gate_sb = {}
         pieces = [(e, g) for e in range(E) for g in range(PASSES)]
@@ -65,29 +65,36 @@ def tile_routed_moe_kernel(tc, xT, w, gate, offs, out):
                 if i == GATE_AT[h]:
                     order.extend([("gate", m, h) for m in range(BLOCKS)])
             order.append(("w",) + pieces[i])
+        first = True
         for kind, a, b in order:
             if kind == "x":
-                planes[a, b] = held.tile([P, T], F32, name="plane%d%d" % (a, b))
-                nc.sync.dma_start(planes[a, b][:], x_view[a, :, b, :])
-                if len(planes) == 1:
+                if a == 0:
+                    nc.sync.dma_start(vector_planes[:, PACK - 1 - b, :], x_view[a, :, b, :])
+                else:
+                    scalar_planes[b] = held.tile([P, T], F32, name="scalar_plane%d" % b)
+                    nc.sync.dma_start(scalar_planes[b][:], x_view[a, :, b, :])
+                if first:
                     nc.sync.dma_start(offsets[:], offs)
+                    first = False
             elif kind == "w":
-                w_raw[a, b] = held.tile([P, PACK, N], F32, name="w_raw%d%d" % (a, b), align_bytes=64)
-                nc.sync.dma_start(w_raw[a, b][:], w_view[a, b])
+                if a in WHOLE_EXPERTS:
+                    if b == 0:
+                        w_raw[a] = held.tile([P, PASSES, PACK, N], F32, name="w_raw%d" % a, align_bytes=64)
+                    nc.sync.dma_start(w_raw[a][:, b, :, :], w_view[a, b])
+                else:
+                    w_raw[a, b] = held.tile([P, PACK, N], F32, name="w_raw%d%d" % (a, b), align_bytes=64)
+                    nc.sync.dma_start(w_raw[a, b][:], w_view[a, b])
             else:
                 gate_sb[a, b] = held.tile([P, HALF], F32, name="gate%d%d" % (a, b))
                 nc.sync.dma_start(gate_sb[a, b][:], gate[a * M_TILE:(a + 1) * M_TILE, b * HALF:(b + 1) * HALF])
 
         x_grouped = {}
-        picked = {}
         x_codes = {}
         x_scales = {}
         for g in range(PASSES):
-            for h in range(HALVES):
-                x_grouped[g, h] = held.tile([P, HALF, PACK], BF16, name="x_grouped%d%d" % (g, h), align_bytes=64)
-                if g != SCALAR_PASS:
-                    picked[g, h] = held.tile([P, PACK, HALF], F32, name="picked%d%d" % (g, h))
-                x_scales[g, h] = held.tile([P, HALF], U8, name="x_scales%d%d" % (g, h), align_bytes=64)
+            x_grouped[g] = held.tile([P, SLOTS, PACK], BF16, name="x_grouped%d" % g, align_bytes=64)
+            x_scales[g] = held.tile([P, SLOTS], U8, name="x_scales%d" % g, align_bytes=64)
+        picked = held.tile([P, PACK, SLOTS], F32, name="picked")
         w_grouped = {}
         w_codes = {}
         w_scales = {}
@@ -95,59 +102,73 @@ def tile_routed_moe_kernel(tc, xT, w, gate, offs, out):
         for m in range(BLOCKS):
             window[m] = held.tile([P, T], F32, name="window%d" % m)
 
-        def half_list(h):
-            return offsets[:, h * HALF // LIST_COL:(h + 1) * HALF // LIST_COL]
+        def slots_list(lo, hi):
+            return offsets[:, lo // LIST_COL:hi // LIST_COL]
 
-        def scalar_plane(g, t):
-            rounded = held.tile([P, T], BF16, name="rounded%d%d" % (g, t))
-            cut = T - SCALAR_SHARE.get((g, t), 0)
+        def scalar_plane(t):
+            rounded = held.tile([P, T], BF16, name="rounded%d" % t)
+            cut = T - SCALAR_SHARE.get((1, t), 0)
             if cut > 0:
-                nc.gpsimd.tensor_copy(out=rounded[:, 0:cut], in_=planes[g, t][:, 0:cut])
+                nc.gpsimd.tensor_copy(out=rounded[:, 0:cut], in_=scalar_planes[t][:, 0:cut])
             if cut < T:
-                nc.scalar.copy(out=rounded[:, cut:T], in_=planes[g, t][:, cut:T])
+                nc.scalar.copy(out=rounded[:, cut:T], in_=scalar_planes[t][:, cut:T])
             for h in range(HALVES):
                 nc.scalar.activation(
-                    x_grouped[g, h][:, :, t],
-                    rounded[:].indirect(half_list(h)),
+                    x_grouped[1][:, h * HALF:(h + 1) * HALF, t],
+                    rounded[:].indirect(slots_list(h * HALF, (h + 1) * HALF)),
                     mybir.ActivationFunctionType.Copy,
                 )
 
-        def vector_plane(g, t):
-            for h in range(HALVES):
-                nc.vector.tensor_copy(picked[g, h][:, t, :], planes[g, t][:].indirect(half_list(h)))
+        def vector_plane(t):
+            at = PACK - 1 - t
+            if t == 0 or not LONG_GATHERS:
+                for h in range(HALVES):
+                    nc.vector.tensor_copy(
+                        picked[:, t, h * HALF:(h + 1) * HALF],
+                        vector_planes[:, at, :].indirect(slots_list(h * HALF, (h + 1) * HALF)),
+                    )
+            else:
+                nc.vector.tensor_copy(
+                    picked[:, t, :],
+                    vector_planes[:, at:at + 2, :].rearrange("p t n -> p (t n)").indirect(offsets[:]),
+                )
 
-        def interleave_tokens(g, h):
-            dst, src = interleaved(x_grouped[g, h][:], picked[g, h][:])
-            nc.vector.tensor_copy(out=dst, in_=src)
+        def quantize_tokens(g, name, cuts):
+            x_codes[g] = held.tile([P, SLOTS], U32, name=name, align_bytes=64)
+            for lo, hi in cuts:
+                nc.vector.quantize_mx(
+                    out=x_codes[g][:, lo:hi].bitcast(FP8X4),
+                    scales=x_scales[g][:, lo:hi],
+                    in_=x_grouped[g][:, lo:hi, :].rearrange("p n t -> p (n t)"),
+                )
 
-        def quantize_tokens(g, h, name):
-            x_codes[g, h] = held.tile([P, HALF], U32, name=name, align_bytes=64)
-            nc.vector.quantize_mx(
-                out=x_codes[g, h][:].bitcast(FP8X4),
-                scales=x_scales[g, h][:],
-                in_=x_grouped[g, h][:].rearrange("p n t -> p (n t)"),
-            )
+        def group_of(e):
+            return [k for k in range(len(GROUPS)) if GROUPS[k][0] <= e < GROUPS[k][1]][0]
 
         def weights(e, g):
-            if g == 0:
-                if e in EARLY_EXPERTS:
-                    w_grouped[e] = held.tile([P, PASSES, N, PACK], BF16, name="w_grouped%d" % e, align_bytes=64)
-                else:
-                    w_grouped[e] = ring.tile([P, PASSES, N, PACK], BF16, name="w_grouped", align_bytes=64)
-            dst, src = interleaved(w_grouped[e][:, g, :, :], w_raw[e, g][:])
-            if (e, g) in VECTOR_WEIGHTS:
-                nc.vector.tensor_copy(out=dst, in_=src)
-            elif (e, g) in GPSIMD_WEIGHTS:
-                nc.gpsimd.tensor_copy(out=w_grouped[e][:, g, :, :], in_=w_raw[e, g][:].rearrange("p j n -> p n j"))
+            k = group_of(e)
+            e0, e1 = GROUPS[k]
+            if e == e0 and g == 0:
+                w_grouped[k] = held.tile([P, e1 - e0, PASSES, N, PACK], BF16, name="w_grouped%d" % k, align_bytes=64)
+            if e in WHOLE_EXPERTS:
+                if g == PASSES - 1:
+                    nc.vector.tensor_copy(
+                        out=w_grouped[k][:, e - e0, :, :, :].rearrange("p g (c i) j -> p g c j i", i=4),
+                        in_=w_raw[e][:].rearrange("p g j (c i) -> p g c j i", i=4),
+                    )
             else:
-                nc.scalar.copy(out=dst, in_=src)
-            if g == PASSES - 1:
-                w_codes[e] = held.tile([P, PASSES * N], U32, name="w_codes%d" % e, align_bytes=64)
-                w_scales[e] = held.tile([P, PASSES * N], U8, name="w_scales%d" % e, align_bytes=64)
+                dst, src = interleaved(w_grouped[k][:, e - e0, g, :, :], w_raw[e, g][:])
+                if (e, g) in VECTOR_PIECES:
+                    nc.vector.tensor_copy(out=dst, in_=src)
+                else:
+                    nc.scalar.copy(out=dst, in_=src)
+            if g == PASSES - 1 and e == e1 - 1:
+                w_codes[k] = held.tile([P, (e1 - e0) * PASSES * N], U32, name="w_codes%d" % k, align_bytes=64)
+                w_scales[k] = held.tile([P, (e1 - e0) * PASSES * N], U8, name="w_scales%d" % k, align_bytes=64)
                 nc.vector.quantize_mx(
-                    out=w_codes[e][:].bitcast(FP8X4),
-                    scales=w_scales[e][:],
-                    in_=w_grouped[e][:].rearrange("p g n j -> p (g n j)"),
+                    out=w_codes[k][:].bitcast(FP8X4),
+                    scales=w_scales[k][:],
+                    in_=w_grouped[k][:].rearrange("p e g n j -> p (e g n j)"),
                 )
 
         def finish(u, m):
@@ -155,49 +176,48 @@ def tile_routed_moe_kernel(tc, xT, w, gate, offs, out):
             slots = (e1 - e0) * C
             acc = psum.tile([P, slots], F32, name="acc%d%d" % (u % 4, m))
             for e in range(e0, e1):
+                k = group_of(e)
                 for g in range(PASSES):
-                    h, col = (e * C) // HALF, (e * C) % HALF
-                    first = g * N + m * M_TILE
+                    first = ((e - GROUPS[k][0]) * PASSES + g) * N + m * M_TILE
                     nc.tensor.matmul_mx(
                         out=acc[:, (e - e0) * C:(e - e0 + 1) * C],
-                        lhsT=w_codes[e][:, first:first + M_TILE].bitcast(FP8X4),
-                        lhsT_scale=w_scales[e][:, first:first + M_TILE],
-                        rhs=x_codes[g, h][:, col:col + C].bitcast(FP8X4),
-                        rhs_scale=x_scales[g, h][:, col:col + C],
+                        lhsT=w_codes[k][:, first:first + M_TILE].bitcast(FP8X4),
+                        lhsT_scale=w_scales[k][:, first:first + M_TILE],
+                        rhs=x_codes[g][:, e * C:(e + 1) * C].bitcast(FP8X4),
+                        rhs_scale=x_scales[g][:, e * C:(e + 1) * C],
                         start=(g == 0),
                         stop=(g == PASSES - 1),
                     )
-            at = SUMS_AT[u] + m
-            name = "w_raw%d%d" % pieces[at] if at < len(pieces) else "sums%d" % m
+            at = SUMS_AT[u][m]
+            name = "w_raw%d%d" % pieces[at] if at < len(pieces) else "sums%d%d" % (u, m)
             sums = held.tile([P, slots], F32, name=name, align_bytes=64)
             nc.scalar.copy(out=sums[:], in_=acc[:])
+            col = e0 * C % HALF
             nc.vector.tensor_tensor(
-                out=window[m][:].indirect(offsets[:, e0 * C // LIST_COL:e1 * C // LIST_COL]),
+                out=window[m][:].indirect(slots_list(e0 * C, e1 * C)),
                 in0=sums[:],
-                in1=gate_sb[m, e0 * C // HALF][:, e0 * C % HALF:e0 * C % HALF + slots],
+                in1=gate_sb[m, e0 * C // HALF][:, col:col + slots],
                 op=mult,
             )
             if e1 == E:
                 nc.sync.dma_start(out=out[m * M_TILE:(m + 1) * M_TILE, :], in_=window[m][:])
 
         for g, t in PLANES:
-            if g == SCALAR_PASS:
-                scalar_plane(g, t)
+            if g == 1:
+                scalar_plane(t)
             else:
-                vector_plane(g, t)
-        for h in range(HALVES):
-            interleave_tokens(0, h)
-        for h in range(HALVES):
-            quantize_tokens(0, h, "x_codes0%d" % h)
+                vector_plane(t)
+        for lo, hi in TOKEN_CUTS:
+            dst, src = interleaved(x_grouped[0][:, lo:hi, :], picked[:, :, lo:hi])
+            nc.vector.tensor_copy(out=dst, in_=src)
+        quantize_tokens(0, "x_codes0", TOKEN_CUTS)
 
         for i in range(len(pieces) + BLOCKS):
             if i < len(pieces):
-                e, g = pieces[i]
-                weights(e, g)
-            for h in range(HALVES):
-                if LATE_AT[h][0] == i:
-                    quantize_tokens(1, h, LATE_AT[h][1])
+                weights(pieces[i][0], pieces[i][1])
+            if LATE_AT[0][0] == i:
+                quantize_tokens(1, LATE_AT[0][1], LATE_CUTS)
             for u in range(len(UNITS)):
                 for m in range(BLOCKS):
-                    if SUMS_AT[u] + m == i:
+                    if SUMS_AT[u][m] == i:
                         finish(u, m)

@@ -23,18 +23,17 @@ LIST_COL = 16
 HALF = 512
 HALVES = SLOTS // HALF
 
-UNITS = ((0, 2), (2, 4), (4, 6), (6, 7), (7, 8))
-GROUPS = ((0, 2), (2, 4), (4, 6), (6, 7), (7, 8))
-SUMS_AT = ((6, 7), (9, 11), (12, 13), (14, 15), (16, 17))
+UNITS = (((0, 2), (2, 4), (4, 6), (6, 7), (7, 8)), ((0, 3), (3, 4), (4, 6), (6, 8)))
+GROUPS = ((0, 1), (1, 2), (2, 3), (3, 4), (4, 6), (6, 7), (7, 8))
+SUMS_AT = ((6, 9, 12, 15, 16), (7, 11, 13, 17))
 PLANES = ((0, 0), (1, 0), (0, 1), (1, 1), (0, 2), (1, 2), (0, 3), (1, 3))
 SCALAR_SHARE = {(1, 0): 512}
-WHOLE_EXPERTS = (0, 1)
-VECTOR_PIECES = ((2, 0),)
+VECTOR_EXPERTS = (0,)
+VECTOR_PIECES = ((3, 1),)
 GATE_AT = (8, 12)
-LATE_AT = ((3, "w_raw1"),)
+MERGE_ENGINE = ("vector", "vector")
+LATE_AT = 0
 LONG_GATHERS = True
-TOKEN_CUTS = ((0, 1024),)
-LATE_CUTS = ((0, 512), (512, 1024))
 
 
 def interleaved(dst, src):
@@ -77,7 +76,7 @@ def tile_routed_moe_kernel(tc, xT, w, gate, offs, out):
                     nc.sync.dma_start(offsets[:], offs)
                     first = False
             elif kind == "w":
-                if a in WHOLE_EXPERTS:
+                if a in VECTOR_EXPERTS:
                     if b == 0:
                         w_raw[a] = held.tile([P, PASSES, PACK, N], F32, name="w_raw%d" % a, align_bytes=64)
                     nc.sync.dma_start(w_raw[a][:, b, :, :], w_view[a, b])
@@ -94,7 +93,9 @@ def tile_routed_moe_kernel(tc, xT, w, gate, offs, out):
         for g in range(PASSES):
             x_grouped[g] = held.tile([P, SLOTS, PACK], BF16, name="x_grouped%d" % g, align_bytes=64)
             x_scales[g] = held.tile([P, SLOTS], U8, name="x_scales%d" % g, align_bytes=64)
-        picked = held.tile([P, PACK, SLOTS], F32, name="picked")
+        paired = {}
+        for g in range(PASSES):
+            paired[g] = held.tile([P, 2, SLOTS, 2], BF16, name="paired%d" % g, align_bytes=64)
         w_grouped = {}
         w_codes = {}
         w_scales = {}
@@ -105,17 +106,19 @@ def tile_routed_moe_kernel(tc, xT, w, gate, offs, out):
         def slots_list(lo, hi):
             return offsets[:, lo // LIST_COL:hi // LIST_COL]
 
+        rounded = {}
+
         def scalar_plane(t):
-            rounded = held.tile([P, T], BF16, name="rounded%d" % t)
+            rounded[t] = held.tile([P, T], BF16, name="rounded%d" % t)
             cut = T - SCALAR_SHARE.get((1, t), 0)
             if cut > 0:
-                nc.gpsimd.tensor_copy(out=rounded[:, 0:cut], in_=scalar_planes[t][:, 0:cut])
+                nc.gpsimd.tensor_copy(out=rounded[t][:, 0:cut], in_=scalar_planes[t][:, 0:cut])
             if cut < T:
-                nc.scalar.copy(out=rounded[:, cut:T], in_=scalar_planes[t][:, cut:T])
+                nc.scalar.copy(out=rounded[t][:, cut:T], in_=scalar_planes[t][:, cut:T])
             for h in range(HALVES):
                 nc.scalar.activation(
-                    x_grouped[1][:, h * HALF:(h + 1) * HALF, t],
-                    rounded[:].indirect(slots_list(h * HALF, (h + 1) * HALF)),
+                    paired[1][:, t // 2, h * HALF:(h + 1) * HALF, t % 2],
+                    rounded[t][:].indirect(slots_list(h * HALF, (h + 1) * HALF)),
                     mybir.ActivationFunctionType.Copy,
                 )
 
@@ -124,33 +127,40 @@ def tile_routed_moe_kernel(tc, xT, w, gate, offs, out):
             if t == 0 or not LONG_GATHERS:
                 for h in range(HALVES):
                     nc.vector.tensor_copy(
-                        picked[:, t, h * HALF:(h + 1) * HALF],
+                        paired[0][:, t // 2, h * HALF:(h + 1) * HALF, t % 2],
                         vector_planes[:, at, :].indirect(slots_list(h * HALF, (h + 1) * HALF)),
                     )
             else:
                 nc.vector.tensor_copy(
-                    picked[:, t, :],
+                    paired[0][:, t // 2, :, t % 2],
                     vector_planes[:, at:at + 2, :].rearrange("p t n -> p (t n)").indirect(offsets[:]),
                 )
 
-        def quantize_tokens(g, name, cuts):
-            x_codes[g] = held.tile([P, SLOTS], U32, name=name, align_bytes=64)
-            for lo, hi in cuts:
-                nc.vector.quantize_mx(
-                    out=x_codes[g][:, lo:hi].bitcast(FP8X4),
-                    scales=x_scales[g][:, lo:hi],
-                    in_=x_grouped[g][:, lo:hi, :].rearrange("p n t -> p (n t)"),
-                )
+        def quantize_tokens(g, lo, hi):
+            nc.vector.quantize_mx(
+                out=x_codes[g][:, lo:hi].bitcast(FP8X4),
+                scales=x_scales[g][:, lo:hi],
+                in_=x_grouped[g][:, lo:hi, :].rearrange("p n t -> p (n t)"),
+            )
+
+        def merge(g):
+            words = paired[g][:].rearrange("p q n r -> p (q n r)").bitcast(F32).rearrange("p (q n) -> p q n", q=2)
+            dst = x_grouped[g][:].rearrange("p n t -> p (n t)").bitcast(F32).rearrange("p (c i q) -> p c q i", i=4, q=2)
+            src = words.rearrange("p q (c i) -> p c q i", i=4)
+            if MERGE_ENGINE[g] == "vector":
+                nc.vector.tensor_copy(out=dst, in_=src)
+            else:
+                nc.scalar.copy(out=dst, in_=src)
 
         def group_of(e):
             return [k for k in range(len(GROUPS)) if GROUPS[k][0] <= e < GROUPS[k][1]][0]
 
-        def weights(e, g):
+        def interleave_weights(e, g):
             k = group_of(e)
             e0, e1 = GROUPS[k]
             if e == e0 and g == 0:
                 w_grouped[k] = held.tile([P, e1 - e0, PASSES, N, PACK], BF16, name="w_grouped%d" % k, align_bytes=64)
-            if e in WHOLE_EXPERTS:
+            if e in VECTOR_EXPERTS:
                 if g == PASSES - 1:
                     nc.vector.tensor_copy(
                         out=w_grouped[k][:, e - e0, :, :, :].rearrange("p g (c i) j -> p g c j i", i=4),
@@ -162,6 +172,9 @@ def tile_routed_moe_kernel(tc, xT, w, gate, offs, out):
                     nc.vector.tensor_copy(out=dst, in_=src)
                 else:
                     nc.scalar.copy(out=dst, in_=src)
+        def quantize_weights(e, g):
+            k = group_of(e)
+            e0, e1 = GROUPS[k]
             if g == PASSES - 1 and e == e1 - 1:
                 w_codes[k] = held.tile([P, (e1 - e0) * PASSES * N], U32, name="w_codes%d" % k, align_bytes=64)
                 w_scales[k] = held.tile([P, (e1 - e0) * PASSES * N], U8, name="w_scales%d" % k, align_bytes=64)
@@ -172,7 +185,7 @@ def tile_routed_moe_kernel(tc, xT, w, gate, offs, out):
                 )
 
         def finish(u, m):
-            e0, e1 = UNITS[u]
+            e0, e1 = UNITS[m][u]
             slots = (e1 - e0) * C
             acc = psum.tile([P, slots], F32, name="acc%d%d" % (u % 4, m))
             for e in range(e0, e1):
@@ -188,7 +201,7 @@ def tile_routed_moe_kernel(tc, xT, w, gate, offs, out):
                         start=(g == 0),
                         stop=(g == PASSES - 1),
                     )
-            at = SUMS_AT[u][m]
+            at = SUMS_AT[m][u]
             name = "w_raw%d%d" % pieces[at] if at < len(pieces) else "sums%d%d" % (u, m)
             sums = held.tile([P, slots], F32, name=name, align_bytes=64)
             nc.scalar.copy(out=sums[:], in_=acc[:])
@@ -207,17 +220,20 @@ def tile_routed_moe_kernel(tc, xT, w, gate, offs, out):
                 scalar_plane(t)
             else:
                 vector_plane(t)
-        for lo, hi in TOKEN_CUTS:
-            dst, src = interleaved(x_grouped[0][:, lo:hi, :], picked[:, :, lo:hi])
-            nc.vector.tensor_copy(out=dst, in_=src)
-        quantize_tokens(0, "x_codes0", TOKEN_CUTS)
+        merge(0)
+        x_codes[0] = held.tile([P, SLOTS], U32, name="x_codes0", align_bytes=64)
+        quantize_tokens(0, 0, SLOTS)
 
         for i in range(len(pieces) + BLOCKS):
             if i < len(pieces):
-                weights(pieces[i][0], pieces[i][1])
-            if LATE_AT[0][0] == i:
-                quantize_tokens(1, LATE_AT[0][1], LATE_CUTS)
-            for u in range(len(UNITS)):
-                for m in range(BLOCKS):
-                    if SUMS_AT[u][m] == i:
+                interleave_weights(pieces[i][0], pieces[i][1])
+            if i == LATE_AT:
+                merge(1)
+                x_codes[1] = held.tile([P, SLOTS], U32, name="x_codes1", align_bytes=64)
+                quantize_tokens(1, 0, SLOTS)
+            if i < len(pieces):
+                quantize_weights(pieces[i][0], pieces[i][1])
+            for m in range(BLOCKS):
+                for u in range(len(UNITS[m])):
+                    if SUMS_AT[m][u] == i:
                         finish(u, m)

@@ -23,8 +23,8 @@ LIST_COL = 16
 HALF = 512
 HALVES = SLOTS // HALF
 
-UNITS = (((0, 2), (2, 4), (4, 6), (6, 7), (7, 8)), ((0, 3), (3, 4), (4, 6), (6, 8)))
-GROUPS = ((0, 1), (1, 2), (2, 3), (3, 4), (4, 6), (6, 7), (7, 8))
+UNITS = (((0, 2), (2, 4), (4, 6), (6, 7), (7, 8)), ((0, 2), (2, 4), (4, 6), (6, 8)))
+GROUPS = ((0, 2), (2, 3), (3, 4), (4, 6), (6, 7), (7, 8))
 SUMS_AT = ((6, 9, 12, 15, 16), (7, 11, 13, 17))
 PLANES = ((0, 0), (1, 0), (0, 1), (1, 1), (0, 2), (1, 2), (0, 3), (1, 3))
 SCALAR_SHARE = {(1, 0): 512}

@@ -145,8 +145,8 @@ def tile_routed_moe_kernel(tc, xT, w, gate, offs, out):
 
         def merge(g):
             words = paired[g][:].rearrange("p q n r -> p (q n r)").bitcast(F32).rearrange("p (q n) -> p q n", q=2)
-            dst = x_grouped[g][:].rearrange("p n t -> p (n t)").bitcast(F32).rearrange("p (c i q) -> p c q i", i=4, q=2)
-            src = words.rearrange("p q (c i) -> p c q i", i=4)
+            dst = x_grouped[g][:].rearrange("p n t -> p (n t)").bitcast(F32).rearrange("p (n q) -> p n q", q=2)
+            src = words.rearrange("p q n -> p n q")
             if MERGE_ENGINE[g] == "vector":
                 nc.vector.tensor_copy(out=dst, in_=src)
             else:

from contextlib import ExitStack

import concourse.mybir as mybir

K, T, E, C, N = 1024, 1024, 8, 128, 256
FLOPS = 2 * K * N * E * C

F32 = mybir.dt.float32
BF16 = mybir.dt.bfloat16
U32 = mybir.dt.uint32
U16 = mybir.dt.uint16
U8 = mybir.dt.uint8
FP8X4 = mybir.dt.float8_e4m3fn_x4

P = 128
PACK = 4
K_PASS = P * PACK
PASSES = K // K_PASS
M_TILE = 128
BLOCKS = N // M_TILE
SLOTS = E * C
LIST_COL = 16
HALF = 512
HALVES = SLOTS // HALF

UNITS = (((0, 2), (2, 4), (4, 6), (6, 7), (7, 8)), ((0, 2), (2, 4), (4, 6), (6, 8)))
GROUPS = ((0, 2), (2, 3), (3, 4), (4, 6), (6, 7), (7, 8))
SUMS_AT = ((6, 9, 12, 15, 16), (7, 11, 13, 17))
PLANES = ((0, 0), (1, 0), (0, 1), (1, 1), (0, 2), (1, 2), (0, 3), (1, 3))
SCALAR_SHARE = {(1, 0): 512}
VECTOR_EXPERTS = (0,)
VECTOR_PIECES = ((3, 1),)
GATE_AT = (8, 12)
MERGE_ENGINE = ("vector", "vector")
LATE_AT = 0
LONG_GATHERS = True


def interleaved(dst, src):
    return dst.rearrange("p (c i) j -> p c j i", i=4), src.rearrange("p j (c i) -> p c j i", i=4)


def tile_routed_moe_kernel(tc, xT, w, gate, offs, out):
    nc = tc.nc
    mult = mybir.AluOpType.mult

    with ExitStack() as ctx:
        held = ctx.enter_context(tc.tile_pool(name="held", bufs=1))
        psum = ctx.enter_context(tc.psum_pool(name="psum", bufs=1))

        offsets = held.tile([P, SLOTS // LIST_COL], U16, name="offsets")

        x_view = xT.rearrange("(g p t) n -> g p t n", p=P, t=PACK)
        w_view = w.rearrange("e (g p j) n -> e g p j n", p=P, j=PACK)

        vector_planes = held.tile([P, PACK, T], F32, name="vector_planes")
        scalar_planes = {}
        w_raw = {}
        gate_sb = {}
        pieces = [(e, g) for e in range(E) for g in range(PASSES)]
        order = [("x",) + p for p in PLANES]
        for i in range(len(pieces)):
            for h in range(HALVES):
                if i == GATE_AT[h]:
                    order.extend([("gate", m, h) for m in range(BLOCKS)])
            order.append(("w",) + pieces[i])
        first = True
        for kind, a, b in order:
            if kind == "x":
                if a == 0:
                    nc.sync.dma_start(vector_planes[:, PACK - 1 - b, :], x_view[a, :, b, :])
                else:
                    scalar_planes[b] = held.tile([P, T], F32, name="scalar_plane%d" % b)
                    nc.sync.dma_start(scalar_planes[b][:], x_view[a, :, b, :])
                if first:
                    nc.sync.dma_start(offsets[:], offs)
                    first = False
            elif kind == "w":
                if a in VECTOR_EXPERTS:
                    if b == 0:
                        w_raw[a] = held.tile([P, PASSES, PACK, N], F32, name="w_raw%d" % a, align_bytes=64)
                    nc.sync.dma_start(w_raw[a][:, b, :, :], w_view[a, b])
                else:
                    w_raw[a, b] = held.tile([P, PACK, N], F32, name="w_raw%d%d" % (a, b), align_bytes=64)
                    nc.sync.dma_start(w_raw[a, b][:], w_view[a, b])
            else:
                gate_sb[a, b] = held.tile([P, HALF], F32, name="gate%d%d" % (a, b))
                nc.sync.dma_start(gate_sb[a, b][:], gate[a * M_TILE:(a + 1) * M_TILE, b * HALF:(b + 1) * HALF])

        x_grouped = {}
        x_codes = {}
        x_scales = {}
        for g in range(PASSES):
            x_grouped[g] = held.tile([P, SLOTS, PACK], BF16, name="x_grouped%d" % g, align_bytes=64)
            x_scales[g] = held.tile([P, SLOTS], U8, name="x_scales%d" % g, align_bytes=64)
        paired = {}
        for g in range(PASSES):
            paired[g] = held.tile([P, 2, SLOTS, 2], BF16, name="paired%d" % g, align_bytes=64)
        w_grouped = {}
        w_codes = {}
        w_scales = {}
        window = {}
        for m in range(BLOCKS):
            window[m] = held.tile([P, T], F32, name="window%d" % m)

        def slots_list(lo, hi):
            return offsets[:, lo // LIST_COL:hi // LIST_COL]

        rounded = {}

        def scalar_plane(t):
            rounded[t] = held.tile([P, T], BF16, name="rounded%d" % t)
            cut = T - SCALAR_SHARE.get((1, t), 0)
            if cut > 0:
                nc.gpsimd.tensor_copy(out=rounded[t][:, 0:cut], in_=scalar_planes[t][:, 0:cut])
            if cut < T:
                nc.scalar.copy(out=rounded[t][:, cut:T], in_=scalar_planes[t][:, cut:T])
            for h in range(HALVES):
                nc.scalar.activation(
                    paired[1][:, t // 2, h * HALF:(h + 1) * HALF, t % 2],
                    rounded[t][:].indirect(slots_list(h * HALF, (h + 1) * HALF)),
                    mybir.ActivationFunctionType.Copy,
                )

        def vector_plane(t):
            at = PACK - 1 - t
            if t == 0 or not LONG_GATHERS:
                for h in range(HALVES):
                    nc.vector.tensor_copy(
                        paired[0][:, t // 2, h * HALF:(h + 1) * HALF, t % 2],
                        vector_planes[:, at, :].indirect(slots_list(h * HALF, (h + 1) * HALF)),
                    )
            else:
                nc.vector.tensor_copy(
                    paired[0][:, t // 2, :, t % 2],
                    vector_planes[:, at:at + 2, :].rearrange("p t n -> p (t n)").indirect(offsets[:]),
                )

        def quantize_tokens(g, lo, hi):
            nc.vector.quantize_mx(
                out=x_codes[g][:, lo:hi].bitcast(FP8X4),
                scales=x_scales[g][:, lo:hi],
                in_=x_grouped[g][:, lo:hi, :].rearrange("p n t -> p (n t)"),
            )

        def merge(g):
            words = paired[g][:].rearrange("p q n r -> p (q n r)").bitcast(F32).rearrange("p (q n) -> p q n", q=2)
            dst = x_grouped[g][:].rearrange("p n t -> p (n t)").bitcast(F32).rearrange("p (n q) -> p n q", q=2)
            src = words.rearrange("p q n -> p n q")
            if MERGE_ENGINE[g] == "vector":
                nc.vector.tensor_copy(out=dst, in_=src)
            else:
                nc.scalar.copy(out=dst, in_=src)

        def group_of(e):
            return [k for k in range(len(GROUPS)) if GROUPS[k][0] <= e < GROUPS[k][1]][0]

        def interleave_weights(e, g):
            k = group_of(e)
            e0, e1 = GROUPS[k]
            if e == e0 and g == 0:
                w_grouped[k] = held.tile([P, e1 - e0, PASSES, N, PACK], BF16, name="w_grouped%d" % k, align_bytes=64)
            if e in VECTOR_EXPERTS:
                if g == PASSES - 1:
                    nc.vector.tensor_copy(
                        out=w_grouped[k][:, e - e0, :, :, :].rearrange("p g (c i) j -> p g c j i", i=4),
                        in_=w_raw[e][:].rearrange("p g j (c i) -> p g c j i", i=4),
                    )
            else:
                dst, src = interleaved(w_grouped[k][:, e - e0, g, :, :], w_raw[e, g][:])
                if (e, g) in VECTOR_PIECES:
                    nc.vector.tensor_copy(out=dst, in_=src)
                else:
                    nc.scalar.copy(out=dst, in_=src)
        def quantize_weights(e, g):
            k = group_of(e)
            e0, e1 = GROUPS[k]
            if g == PASSES - 1 and e == e1 - 1:
                w_codes[k] = held.tile([P, (e1 - e0) * PASSES * N], U32, name="w_codes%d" % k, align_bytes=64)
                w_scales[k] = held.tile([P, (e1 - e0) * PASSES * N], U8, name="w_scales%d" % k, align_bytes=64)
                nc.vector.quantize_mx(
                    out=w_codes[k][:].bitcast(FP8X4),
                    scales=w_scales[k][:],
                    in_=w_grouped[k][:].rearrange("p e g n j -> p (e g n j)"),
                )

        def finish(u, m):
            e0, e1 = UNITS[m][u]
            slots = (e1 - e0) * C
            acc = psum.tile([P, slots], F32, name="acc%d%d" % (u % 4, m))
            for e in range(e0, e1):
                k = group_of(e)
                for g in range(PASSES):
                    first = ((e - GROUPS[k][0]) * PASSES + g) * N + m * M_TILE
                    nc.tensor.matmul_mx(
                        out=acc[:, (e - e0) * C:(e - e0 + 1) * C],
                        lhsT=w_codes[k][:, first:first + M_TILE].bitcast(FP8X4),
                        lhsT_scale=w_scales[k][:, first:first + M_TILE],
                        rhs=x_codes[g][:, e * C:(e + 1) * C].bitcast(FP8X4),
                        rhs_scale=x_scales[g][:, e * C:(e + 1) * C],
                        start=(g == 0),
                        stop=(g == PASSES - 1),
                    )
            at = SUMS_AT[m][u]
            name = "w_raw%d%d" % pieces[at] if at < len(pieces) else "sums%d%d" % (u, m)
            sums = held.tile([P, slots], F32, name=name, align_bytes=64)
            nc.scalar.copy(out=sums[:], in_=acc[:])
            col = e0 * C % HALF
            nc.vector.tensor_tensor(
                out=window[m][:].indirect(slots_list(e0 * C, e1 * C)),
                in0=sums[:],
                in1=gate_sb[m, e0 * C // HALF][:, col:col + slots],
                op=mult,
            )
            if e1 == E:
                nc.sync.dma_start(out=out[m * M_TILE:(m + 1) * M_TILE, :], in_=window[m][:])

        for g, t in PLANES:
            if g == 1:
                scalar_plane(t)
            else:
                vector_plane(t)
        merge(0)
        x_codes[0] = held.tile([P, SLOTS], U32, name="x_codes0", align_bytes=64)
        quantize_tokens(0, 0, SLOTS)

        for i in range(len(pieces) + BLOCKS):
            if i < len(pieces):
                interleave_weights(pieces[i][0], pieces[i][1])
            if i == LATE_AT:
                merge(1)
                x_codes[1] = held.tile([P, SLOTS], U32, name="x_codes1", align_bytes=64)
                quantize_tokens(1, 0, SLOTS)
            if i < len(pieces):
                quantize_weights(pieces[i][0], pieces[i][1])
            for m in range(BLOCKS):
                for u in range(len(UNITS[m])):
                    if SUMS_AT[m][u] == i:
                        finish(u, m)
